import numpy as np
import ml_dtypes


def mxq(x, axis, fmt="e4m3"):
    dtype, down = {"e4m3": (ml_dtypes.float8_e4m3fn, 7), "e5m2": (ml_dtypes.float8_e5m2, 14)}[fmt]
    v = np.moveaxis(np.asarray(x, np.float32).astype(ml_dtypes.bfloat16).astype(np.float64), axis, -1)
    blocks = v.reshape(v.shape[:-1] + (-1, 32))
    amax = np.abs(blocks).max(-1, keepdims=True)
    byte = np.maximum(np.where(amax > 0, np.frexp(amax)[1] - 1 + 127, 0) - down, 1)
    scale = np.exp2(byte - 127.0)
    codes = (blocks / scale).astype(np.float32).astype(dtype).astype(np.float64)
    return np.moveaxis((codes * scale).reshape(v.shape), -1, axis)


WIDE = False


def mx_kscale(k):
    if not WIDE:
        return np.ones(k)
    levels = np.array([10, -10, 5, -5, 0])
    if k % 512:
        return np.exp2(np.random.permutation(np.resize(levels, k // 32))).repeat(32)
    a = np.empty((k // 512, 16))
    for p in range(k // 512):
        a[p, :8] = np.random.permutation(np.resize(levels, 8))
        for g in range(8):
            far = levels[np.abs(levels - a[p, g]) >= 10]
            a[p, g + 8] = far[np.random.randint(len(far))]
    return np.exp2(a.ravel()).repeat(32)


def f64(x):
    return np.asarray(x).astype(np.float64)


def striped(idx):
    return np.tile(np.asarray(idx).reshape(-1, 16).T, (8, 1)).astype(np.uint16)


def unstriped(offs):
    return offs[:16].T.reshape(-1).astype(np.int64)


E2M1 = np.array([0.0, 0.5, 1.0, 1.5, 2.0, 3.0, 4.0, 6.0, -0.0, -0.5, -1.0, -1.5, -2.0, -3.0, -4.0, -6.0])


def pack_weight(w, fmt):
    k, n = w.shape
    w = f64(np.asarray(w, np.float32).astype(ml_dtypes.bfloat16)).reshape(k // 32, 32, n)
    amax = np.abs(w).max(1)
    if fmt == "e4m3":
        byte = np.frexp(amax)[1] - 1 + 127 - 7
    else:
        mant, ex = np.frexp(amax / 6.0)
        byte = np.where(mant > 0.5, ex, ex - 1) + 127
    byte = np.clip(np.where(amax > 0, byte, 1), 1, 254)
    scaled = (w * np.exp2(127.0 - byte)[:, None, :]).reshape(k, n).astype(np.float32)
    by_word = np.ascontiguousarray(scaled.reshape(k // 512, 128, 4, n).transpose(0, 1, 3, 2))
    if fmt == "e4m3":
        words = by_word.astype(ml_dtypes.float8_e4m3fn).view(np.uint8)
    else:
        c = by_word.astype(ml_dtypes.float4_e2m1fn).view(np.uint8) & 0xF
        words = (c[..., 0::2] | (c[..., 1::2] << 4)).reshape(k // 512, 128, 2 * n)
    return np.ascontiguousarray(words), np.ascontiguousarray(byte.astype(np.uint8).reshape(k // 512, 16, n))


def unpack_weight(words, scales, fmt):
    g, _, n = scales.shape
    words = np.ascontiguousarray(words).reshape(g, 128, n, -1)
    if fmt == "e4m3":
        vals = words.view(ml_dtypes.float8_e4m3fn).astype(np.float64)
    else:
        nib = np.empty((g, 128, n, 4), np.uint8)
        nib[..., 0::2] = words & 0xF
        nib[..., 1::2] = words >> 4
        vals = E2M1[nib]
    vals = vals * np.repeat(np.exp2(scales.astype(np.float64) - 127.0), 8, axis=1)[..., None]
    return vals.transpose(0, 1, 3, 2).reshape(g * 512, n)


def bf(x):
    return np.asarray(x, np.float32).astype(ml_dtypes.bfloat16)


def planes(Y):
    r, m = Y.shape
    b = f64(bf(Y)).reshape(r // 32, 32, m)
    amax = np.abs(b).max(1)
    byte = np.clip(np.where(amax > 0, np.frexp(amax)[1] - 1 + 127 - 7, 1), 1, 254)
    codes = (b * np.exp2(127.0 - byte)[:, None, :]).reshape(r, m).astype(np.float32).astype(ml_dtypes.float8_e4m3fn).view(np.uint8)
    words = codes.reshape(r // 512, 128, 4, m).transpose(0, 1, 3, 2)
    return np.ascontiguousarray(words), np.ascontiguousarray(byte.astype(np.uint8).reshape(r // 512, 16, m))


D, T, I, J, U, Z, E = 512, 2048, 512, 512, 1024, 1024, 512


def setup_inputs():
    n = np.random.standard_normal
    idx = np.random.permutation(T)[:I]
    idx2 = np.random.permutation(U)[:J]
    idx3 = np.random.permutation(Z)[:J]
    fd = mx_kscale(D)
    fi = mx_kscale(I)
    ti = np.ones(T)
    ti[idx] = fi
    keysp = pack_weight(n((D, T)) / fd[:, None], "e2m1")
    return {
        "keys_words": keysp[0],
        "keys_scales": keysp[1],
        "notes": (n((D, U)) * 1.0 / np.sqrt(D) * fd[:, None]).astype(np.float32),
        "users2": (n((D, Z)) * 1.0 / np.sqrt(D) * fd[:, None]).astype(np.float32),
        "rowf": (np.random.uniform(0.02, 0.08, (I, 1)) * fi[:, None]).astype(np.float32),
        "vals": (n((E, T)) / ti).astype(np.float32),
        "offs": striped(idx),
        "offs2": striped(idx2),
        "offs3": striped(idx3),
    }


def reference(keys_words, keys_scales, notes, users2, rowf, vals, offs, offs2, offs3):
    idx = unstriped(offs)
    idx2 = unstriped(offs2)
    idx3 = unstriped(offs3)
    keysu = unpack_weight(keys_words, keys_scales, "e2m1")
    keysidxg = keysu[:, idx]
    notesidx2q = mxq(f64(notes)[:, idx2], 0, "e4m3")
    g1 = keysidxg.T @ notesidx2q
    users2idx3q = mxq(f64(users2)[:, idx3], 0, "e4m3")
    g2 = keysidxg.T @ users2idx3q
    g0 = np.maximum(g1, g2)
    gr1 = g0 * f64(rowf)
    vt1 = f64(vals)[:, idx].T
    vt1q = mxq(vt1, 0, "e4m3")
    gr1q = mxq(gr1, 0, "e4m3")
    o = vt1q.T @ gr1q
    words, scales = planes(o)
    return o, words, scales

@@ -1,0 +1,271 @@
+from contextlib import ExitStack
+
+import concourse.mybir as mybir
+from concourse.masks import make_identity
+
+D, T, I, J, U, Z, E = 512, 2048, 512, 512, 1024, 1024, 512
+FLOPS = 2 * D * I * J * 2 + 2 * I * E * J
+
+F32 = mybir.dt.float32
+BF16 = mybir.dt.bfloat16
+I32 = mybir.dt.int32
+U32 = mybir.dt.uint32
+U16 = mybir.dt.uint16
+U8 = mybir.dt.uint8
+FP8X4 = mybir.dt.float8_e4m3fn_x4
+FP4X4 = mybir.dt.float4_e2m1fn_x4
+COPY = mybir.ActivationFunctionType.Copy
+MAX = mybir.AluOpType.max
+MULT = mybir.AluOpType.mult
+
+P = 128
+PACK = 4
+H = J // 2
+LINE = 4
+
+
+def tile_attend_tab_larger_exchange_pl_kernel(
+    tc, keys_words, keys_scales, notes, users2, rowf, vals, offs, offs2, offs3, out_0, out_1, out_2
+):
+    nc = tc.nc
+    with ExitStack() as ctx:
+        lists = ctx.enter_context(tc.tile_pool(name="lists", bufs=1))
+        sb = ctx.enter_context(tc.tile_pool(name="sb", bufs=1))
+        ps = ctx.enter_context(tc.psum_pool(name="ps", bufs=1))
+
+        def tile(shape, dtype, name, tag=None):
+            return sb.tile(shape, dtype, name=name, tag=tag or name, align_bytes=64)
+
+        def half(h):
+            return slice(H * h, H * (h + 1))
+
+        def half_list(h):
+            return slice(H // 16 * h, H // 16 * (h + 1))
+
+        tok_list = lists.tile([P, I // 16], U16, name="tok_list")
+        note_list = lists.tile([P, J // 16], U16, name="note_list")
+        user_list = lists.tile([P, J // 16], U16, name="user_list")
+
+        key_words = tile([P, T], U16, "key_words")
+        key_bytes = tile([P, T], U8, "key_bytes")
+        note_win = [tile([P, U], F32, "note_win%d" % t) for t in range(PACK)]
+        user_win = [tile([P, Z], F32, "user_win%d" % t) for t in range(PACK)]
+        val_win = [tile([P, T], F32, "val_win%d" % t) for t in range(PACK)]
+        factor = tile([P, PACK], F32, "factor")
+        ident = tile([P, P], F32, "ident")
+
+        make_identity(nc, ident[:])
+        nc.sync.dma_start(factor[:], rowf.rearrange("(p r) o -> p (r o)", r=PACK))
+        nc.sync.dma_start(tok_list[:], offs)
+        nc.sync.dma_start(key_words[:].bitcast(I32), keys_words[0].bitcast(I32))
+        nc.sync.dma_start(note_list[:], offs2)
+        notes_t = notes.rearrange("(p t) u -> t p u", t=PACK)
+        users_t = users2.rearrange("(p t) z -> t p z", t=PACK)
+        vals_t = vals.rearrange("(m t) k -> t m k", t=PACK)
+        nc.sync.dma_start(note_win[0][:], notes_t[0])
+        for q in range(4):
+            rows = keys_scales[0, 4 * q : 4 * q + 4, :].bitcast(I32)
+            nc.sync.dma_start(key_bytes[32 * q : 32 * q + 32, :].bitcast(I32), rows.partition_broadcast(8))
+        for t in range(1, PACK):
+            nc.sync.dma_start(note_win[t][:], notes_t[t])
+        nc.sync.dma_start(user_list[:], offs3)
+        for t in range(PACK):
+            nc.sync.dma_start(user_win[t][:], users_t[t])
+        for t in range(PACK):
+            nc.sync.dma_start(val_win[t][:], vals_t[t])
+
+        factor_lines = tile([P, PACK, LINE], F32, "factor_lines")
+        nc.scalar.copy(factor_lines[:], factor[:].unsqueeze(2).to_broadcast([P, PACK, LINE]))
+
+        def bank(shape):
+            return ps.tile(shape, F32, name="bank", tag="bank", bufs=8)
+
+        def gather_vector(out, window, offsets):
+            nc.vector.tensor_copy(out, window.indirect(offsets))
+
+        def gather_scalar(out, window, offsets):
+            nc.scalar.activation(out, window.indirect(offsets), COPY)
+
+        def mx_tiles(name, width):
+            return tile([P, width], U32, name + "_codes"), tile([P, width], U8, name + "_scales")
+
+        def quantize(operand, cols, grouped):
+            codes, scales = operand
+            nc.vector.quantize_mx(out=codes[:, cols].bitcast(FP8X4), scales=scales[:, cols], in_=grouped)
+
+        def flat(grouped):
+            return grouped.rearrange("p j t -> p (j t)")
+
+        kw_listed = tile([P, I], U16, "kw_listed")
+        gather_vector(kw_listed[:], key_words[:], tok_list[:])
+        kw = tile([P, I], U16, "kw")
+        nc.vector.tensor_copy(
+            kw[:].rearrange("p (r s) -> p r s", r=PACK), kw_listed[:].rearrange("p (s r) -> p r s", r=PACK)
+        )
+        ks = tile([P, I], U8, "ks")
+        gather_vector(ks[:].rearrange("p (r s) -> p s r", r=PACK), key_bytes[:], tok_list[:])
+
+        def table(out, r, operand, cols):
+            codes, scales = operand
+            rows = slice(P * r, P * (r + 1))
+            nc.tensor.matmul_mx(
+                out,
+                lhsT=kw[:, rows].bitcast(FP4X4),
+                lhsT_scale=ks[:, rows],
+                rhs=codes[:, cols].bitcast(FP8X4),
+                rhs_scale=scales[:, cols],
+                start=True,
+                stop=True,
+            )
+
+        def place(grouped, pair, planes):
+            nc.vector.tensor_copy(grouped[:, :, 2 * pair : 2 * pair + 2], planes.rearrange("p t j -> p j t"))
+
+        note_lo = tile([P, 2, J], BF16, "note_lo")
+        note_hi = tile([P, 2, J], BF16, "note_hi")
+        note_i = tile([P, J, PACK], BF16, "note_i", "key_bytes")
+        note_q = mx_tiles("note", J)
+        gather_scalar(note_lo[:, 0, :], note_win[0][:], note_list[:])
+        gather_scalar(note_lo[:, 1, half(0)], note_win[1][:], note_list[:, half_list(0)])
+        gather_vector(note_lo[:, 1, half(1)], note_win[1][:], note_list[:, half_list(1)])
+        gather_scalar(note_hi[:, 0, :], note_win[2][:], note_list[:])
+        place(note_i, 0, note_lo[:])
+        gather_vector(note_hi[:, 1, half(0)], note_win[3][:], note_list[:, half_list(0)])
+        gather_scalar(note_hi[:, 1, half(1)], note_win[3][:], note_list[:, half_list(1)])
+        place(note_i, 1, note_hi[:])
+        quantize(note_q, slice(0, J), flat(note_i[:]))
+
+        user_lo = [tile([P, 2, H], BF16, "user_lo%d" % h) for h in range(2)]
+        user_hi = [tile([P, 2, H], BF16, "user_hi%d" % h) for h in range(2)]
+        user_i = [tile([P, H, PACK], BF16, "user_i%d" % h) for h in range(2)]
+        user_q = mx_tiles("user", J)
+        for h in range(2):
+            gather_scalar(user_lo[h][:, 0, :], user_win[0][:], user_list[:, half_list(h)])
+        gather_scalar(user_lo[0][:, 1, :], user_win[1][:], user_list[:, half_list(0)])
+        gather_vector(user_lo[1][:, 1, :], user_win[1][:], user_list[:, half_list(1)])
+        g1_banks = []
+        for r in range(PACK):
+            g1_banks.append(bank([P, J]))
+            table(g1_banks[r][:], r, note_q, slice(0, J))
+        for h in range(2):
+            gather_scalar(user_hi[h][:, 0, :], user_win[2][:], user_list[:, half_list(h)])
+        for h in range(2):
+            place(user_i[h], 0, user_lo[h][:])
+        gather_scalar(user_hi[0][:, 1, :], user_win[3][:], user_list[:, half_list(0)])
+        gather_vector(user_hi[1][:, 1, :], user_win[3][:], user_list[:, half_list(1)])
+        g1 = tile([P, PACK, J], F32, "g1", "user_win3")
+        for r in range(PACK):
+            nc.scalar.copy(g1[:, r, :], g1_banks[r][:])
+        for h in range(2):
+            place(user_i[h], 1, user_hi[h][:])
+        for h in range(2):
+            quantize(user_q, half(h), flat(user_i[h][:]))
+
+        turned = {}
+        val_grouped = {}
+        val_q = [mx_tiles("val%d" % t, P) for t in range(PACK)]
+
+        def value_turn(t):
+            listed = tile([P, I], BF16, "val_listed%d" % t)
+            gather_scalar(listed[:], val_win[t][:], tok_list[:])
+            words = listed[:].bitcast(F32)
+            turned[t] = bank([P, 2, P])
+            for u in range(2):
+                nc.tensor.transpose(turned[t][:, u, :], words[:, u : 2 * P : 2], ident[:])
+
+        def value_group(t, copy):
+            val_grouped[t] = tile([P, P * PACK], BF16, "val_grouped%d" % t)
+            copy(
+                val_grouped[t][:].bitcast(F32).rearrange("p (m u) -> p m u", u=2),
+                turned[t][:].rearrange("p u m -> p m u"),
+            )
+
+        def value_quantize(t):
+            quantize(val_q[t], slice(0, P), val_grouped[t][:])
+
+        larger = [tile([P, PACK, H], F32, "larger%d" % h) for h in range(2)]
+        table_i = [tile([P, H, PACK], BF16, "table_i%d" % h) for h in range(2)]
+        table_q = mx_tiles("table", J)
+
+        g2_banks = {}
+        for h in range(2):
+            for pair in range(2):
+                g2_banks[h, pair] = bank([P, 2, H])
+                for k in range(2):
+                    table(g2_banks[h, pair][:, k, :], 2 * pair + k, user_q, half(h))
+
+        def take_larger(h, pair):
+            rows = slice(2 * pair, 2 * pair + 2)
+            nc.vector.tensor_tensor(larger[h][:, rows, :], g2_banks[h, pair][:], g1[:, rows, half(h)], MAX)
+
+        def scale_rows(h):
+            nc.vector.tensor_tensor(
+                table_i[h][:].rearrange("p (c i) r -> p c r i", i=LINE),
+                larger[h][:].rearrange("p r (c i) -> p c r i", i=LINE),
+                factor_lines[:].unsqueeze(1).to_broadcast([P, H // LINE, PACK, LINE]),
+                MULT,
+            )
+
+        def products(planes, h):
+            acc = bank([P, len(planes), H])
+            for k, t in enumerate(planes):
+                nc.tensor.matmul_mx(
+                    acc[:, k, :],
+                    lhsT=val_q[t][0][:].bitcast(FP8X4),
+                    lhsT_scale=val_q[t][1][:],
+                    rhs=table_q[0][:, half(h)].bitcast(FP8X4),
+                    rhs_scale=table_q[1][:, half(h)],
+                    start=True,
+                    stop=True,
+                )
+            return acc
+
+        value_turn(0)
+        take_larger(0, 0)
+        take_larger(0, 1)
+        value_turn(1)
+        value_group(0, nc.scalar.copy)
+        take_larger(1, 0)
+        scale_rows(0)
+        value_group(1, nc.scalar.copy)
+        take_larger(1, 1)
+        value_turn(2)
+        quantize(table_q, half(0), flat(table_i[0][:]))
+        value_quantize(0)
+        value_quantize(1)
+        first = [products([0, 1], 0)]
+        scale_rows(1)
+        value_group(2, nc.vector.tensor_copy)
+        quantize(table_q, half(1), flat(table_i[1][:]))
+        value_quantize(2)
+        value_turn(3)
+        first.append(products([0, 1], 1))
+
+        res_lo = [tile([P, 2, H], F32, "res_lo0", "table_i1"), tile([P, 2, H], F32, "res_lo1")]
+        res_hi = [tile([P, 2, H], F32, "res_hi%d" % h) for h in range(2)]
+        res_i = [tile([P, H, PACK], BF16, "res_i%d" % h) for h in range(2)]
+        res_q = mx_tiles("res", J)
+        out_t = out_0.rearrange("(m t) j -> m t j", t=PACK)
+
+        nc.vector.tensor_copy(res_lo[0][:], first[0][:])
+        nc.sync.dma_start(out_t[:, 0:2, half(0)], res_lo[0][:])
+        place(res_i[0], 0, res_lo[0][:])
+        nc.scalar.copy(res_lo[1][:], first[1][:])
+        nc.sync.dma_start(out_t[:, 0:2, half(1)], res_lo[1][:])
+        value_group(3, nc.scalar.copy)
+        value_quantize(3)
+        third = [products([2], h) for h in range(2)]
+        place(res_i[1], 0, res_lo[1][:])
+        nc.vector.tensor_copy(res_hi[0][:, 0:1, :], third[0][:])
+        nc.scalar.copy(res_hi[1][:, 0:1, :], third[1][:])
+        for h in range(2):
+            last = products([3], h)
+            nc.scalar.copy(res_hi[h][:, 1:2, :], last[:])
+            nc.sync.dma_start(out_t[:, 2:4, half(h)], res_hi[h][:])
+            place(res_i[h], 1, res_hi[h][:])
+        for h in range(2):
+            quantize(res_q, half(h), flat(res_i[h][:]))
+        nc.sync.dma_start(out_1[0].rearrange("p c r -> p (c r)").bitcast(I32), res_q[0][:].bitcast(I32))
+        for r in range(4):
+            queue = nc.sync if r % 2 == 0 else nc.scalar
+            queue.dma_start(out_2[0, r:16:4, :].bitcast(I32), res_q[1][r:P:32, :].bitcast(I32))

@@ -57,15 +57,15 @@ def tile_attend_tab_larger_exchange_pl_kernel(
         make_identity(nc, ident[:])
         nc.sync.dma_start(factor[:], rowf.rearrange("(p r) o -> p (r o)", r=PACK))
         nc.sync.dma_start(tok_list[:], offs)
+        for q in range(4):
+            rows = keys_scales[0, 4 * q : 4 * q + 4, :].bitcast(I32)
+            nc.sync.dma_start(key_bytes[32 * q : 32 * q + 32, :].bitcast(I32), rows.partition_broadcast(8))
         nc.sync.dma_start(key_words[:].bitcast(I32), keys_words[0].bitcast(I32))
-        nc.sync.dma_start(note_list[:], offs2)
         notes_t = notes.rearrange("(p t) u -> t p u", t=PACK)
         users_t = users2.rearrange("(p t) z -> t p z", t=PACK)
         vals_t = vals.rearrange("(m t) k -> t m k", t=PACK)
         nc.sync.dma_start(note_win[0][:], notes_t[0])
-        for q in range(4):
-            rows = keys_scales[0, 4 * q : 4 * q + 4, :].bitcast(I32)
-            nc.sync.dma_start(key_bytes[32 * q : 32 * q + 32, :].bitcast(I32), rows.partition_broadcast(8))
+        nc.sync.dma_start(note_list[:], offs2)
         for t in range(1, PACK):
             nc.sync.dma_start(note_win[t][:], notes_t[t])
         nc.sync.dma_start(user_list[:], offs3)
@@ -77,8 +77,8 @@ def tile_attend_tab_larger_exchange_pl_kernel(
         factor_lines = tile([P, PACK, LINE], F32, "factor_lines")
         nc.scalar.copy(factor_lines[:], factor[:].unsqueeze(2).to_broadcast([P, PACK, LINE]))
 
-        def bank(shape):
-            return ps.tile(shape, F32, name="bank", tag="bank", bufs=8)
+        def bank(shape, b):
+            return ps.tile(shape, F32, name="bank%d" % b, tag="bank%d" % b)
 
         def gather_vector(out, window, offsets):
             nc.vector.tensor_copy(out, window.indirect(offsets))
@@ -86,8 +86,8 @@ def tile_attend_tab_larger_exchange_pl_kernel(
         def gather_scalar(out, window, offsets):
             nc.scalar.activation(out, window.indirect(offsets), COPY)
 
-        def mx_tiles(name, width):
-            return tile([P, width], U32, name + "_codes"), tile([P, width], U8, name + "_scales")
+        def mx_tiles(name, width, tag=None):
+            return tile([P, width], U32, name + "_codes", tag), tile([P, width], U8, name + "_scales")
 
         def quantize(operand, cols, grouped):
             codes, scales = operand
@@ -96,14 +96,14 @@ def tile_attend_tab_larger_exchange_pl_kernel(
         def flat(grouped):
             return grouped.rearrange("p j t -> p (j t)")
 
+        ks = tile([P, I], U8, "ks")
+        gather_vector(ks[:].rearrange("p (r s) -> p s r", r=PACK), key_bytes[:], tok_list[:])
         kw_listed = tile([P, I], U16, "kw_listed")
         gather_vector(kw_listed[:], key_words[:], tok_list[:])
         kw = tile([P, I], U16, "kw")
         nc.vector.tensor_copy(
             kw[:].rearrange("p (r s) -> p r s", r=PACK), kw_listed[:].rearrange("p (s r) -> p r s", r=PACK)
         )
-        ks = tile([P, I], U8, "ks")
-        gather_vector(ks[:].rearrange("p (r s) -> p s r", r=PACK), key_bytes[:], tok_list[:])
 
         def table(out, r, operand, cols):
             codes, scales = operand
@@ -121,18 +121,16 @@ def tile_attend_tab_larger_exchange_pl_kernel(
         def place(grouped, pair, planes):
             nc.vector.tensor_copy(grouped[:, :, 2 * pair : 2 * pair + 2], planes.rearrange("p t j -> p j t"))
 
-        note_lo = tile([P, 2, J], BF16, "note_lo")
-        note_hi = tile([P, 2, J], BF16, "note_hi")
-        note_i = tile([P, J, PACK], BF16, "note_i", "key_bytes")
+        note_g = tile([P, PACK, J], BF16, "note_g")
+        note_i = tile([P, J, PACK], BF16, "note_i")
         note_q = mx_tiles("note", J)
-        gather_scalar(note_lo[:, 0, :], note_win[0][:], note_list[:])
-        gather_scalar(note_lo[:, 1, half(0)], note_win[1][:], note_list[:, half_list(0)])
-        gather_vector(note_lo[:, 1, half(1)], note_win[1][:], note_list[:, half_list(1)])
-        gather_scalar(note_hi[:, 0, :], note_win[2][:], note_list[:])
-        place(note_i, 0, note_lo[:])
-        gather_vector(note_hi[:, 1, half(0)], note_win[3][:], note_list[:, half_list(0)])
-        gather_scalar(note_hi[:, 1, half(1)], note_win[3][:], note_list[:, half_list(1)])
-        place(note_i, 1, note_hi[:])
+        gather_scalar(note_g[:, 0, :], note_win[0][:], note_list[:])
+        for t in range(1, PACK):
+            gather_scalar(note_g[:, t, half(0)], note_win[t][:], note_list[:, half_list(0)])
+            gather_vector(note_g[:, t, half(1)], note_win[t][:], note_list[:, half_list(1)])
+        nc.vector.tensor_copy(
+            note_i[:].rearrange("p (c i) t -> p c t i", i=LINE), note_g[:].rearrange("p t (c i) -> p c t i", i=LINE)
+        )
         quantize(note_q, slice(0, J), flat(note_i[:]))
 
         user_lo = [tile([P, 2, H], BF16, "user_lo%d" % h) for h in range(2)]
@@ -145,7 +143,7 @@ def tile_attend_tab_larger_exchange_pl_kernel(
         gather_vector(user_lo[1][:, 1, :], user_win[1][:], user_list[:, half_list(1)])
         g1_banks = []
         for r in range(PACK):
-            g1_banks.append(bank([P, J]))
+            g1_banks.append(bank([P, J], r))
             table(g1_banks[r][:], r, note_q, slice(0, J))
         for h in range(2):
             gather_scalar(user_hi[h][:, 0, :], user_win[2][:], user_list[:, half_list(h)])
@@ -163,24 +161,25 @@ def tile_attend_tab_larger_exchange_pl_kernel(
 
         turned = {}
         val_grouped = {}
-        val_q = [mx_tiles("val%d" % t, P) for t in range(PACK)]
+        val_q = {}
 
-        def value_turn(t):
+        def value_turn(t, b):
             listed = tile([P, I], BF16, "val_listed%d" % t)
             gather_scalar(listed[:], val_win[t][:], tok_list[:])
             words = listed[:].bitcast(F32)
-            turned[t] = bank([P, 2, P])
+            turned[t] = bank([P, 2, P], b)
             for u in range(2):
                 nc.tensor.transpose(turned[t][:, u, :], words[:, u : 2 * P : 2], ident[:])
 
-        def value_group(t, copy):
-            val_grouped[t] = tile([P, P * PACK], BF16, "val_grouped%d" % t)
-            copy(
+        def value_group(t, tag=None):
+            val_grouped[t] = tile([P, P * PACK], BF16, "val_grouped%d" % t, tag)
+            nc.scalar.copy(
                 val_grouped[t][:].bitcast(F32).rearrange("p (m u) -> p m u", u=2),
                 turned[t][:].rearrange("p u m -> p m u"),
             )
 
-        def value_quantize(t):
+        def value_quantize(t, tag=None):
+            val_q[t] = mx_tiles("val%d" % t, P, tag)
             quantize(val_q[t], slice(0, P), val_grouped[t][:])
 
         larger = [tile([P, PACK, H], F32, "larger%d" % h) for h in range(2)]
@@ -190,7 +189,7 @@ def tile_attend_tab_larger_exchange_pl_kernel(
         g2_banks = {}
         for h in range(2):
             for pair in range(2):
-                g2_banks[h, pair] = bank([P, 2, H])
+                g2_banks[h, pair] = bank([P, 2, H], PACK + 2 * h + pair)
                 for k in range(2):
                     table(g2_banks[h, pair][:, k, :], 2 * pair + k, user_q, half(h))
 
@@ -206,8 +205,8 @@ def tile_attend_tab_larger_exchange_pl_kernel(
                 MULT,
             )
 
-        def products(planes, h):
-            acc = bank([P, len(planes), H])
+        def products(planes, h, b):
+            acc = bank([P, len(planes), H], b)
             for k, t in enumerate(planes):
                 nc.tensor.matmul_mx(
                     acc[:, k, :],
@@ -220,46 +219,42 @@ def tile_attend_tab_larger_exchange_pl_kernel(
                 )
             return acc
 
-        value_turn(0)
-        take_larger(0, 0)
-        take_larger(0, 1)
-        value_turn(1)
-        value_group(0, nc.scalar.copy)
-        take_larger(1, 0)
-        scale_rows(0)
-        value_group(1, nc.scalar.copy)
-        take_larger(1, 1)
-        value_turn(2)
-        quantize(table_q, half(0), flat(table_i[0][:]))
-        value_quantize(0)
-        value_quantize(1)
-        first = [products([0, 1], 0)]
-        scale_rows(1)
-        value_group(2, nc.vector.tensor_copy)
-        quantize(table_q, half(1), flat(table_i[1][:]))
-        value_quantize(2)
-        value_turn(3)
-        first.append(products([0, 1], 1))
-
-        res_lo = [tile([P, 2, H], F32, "res_lo0", "table_i1"), tile([P, 2, H], F32, "res_lo1")]
-        res_hi = [tile([P, 2, H], F32, "res_hi%d" % h) for h in range(2)]
         res_i = [tile([P, H, PACK], BF16, "res_i%d" % h) for h in range(2)]
         res_q = mx_tiles("res", J)
         out_t = out_0.rearrange("(m t) j -> m t j", t=PACK)
 
-        nc.vector.tensor_copy(res_lo[0][:], first[0][:])
-        nc.sync.dma_start(out_t[:, 0:2, half(0)], res_lo[0][:])
-        place(res_i[0], 0, res_lo[0][:])
-        nc.scalar.copy(res_lo[1][:], first[1][:])
-        nc.sync.dma_start(out_t[:, 0:2, half(1)], res_lo[1][:])
-        value_group(3, nc.scalar.copy)
+        value_turn(0, 0)
+        for h in range(2):
+            for pair in range(2):
+                take_larger(h, pair)
+        value_turn(1, 1)
+        value_group(0, "val_win1")
+        value_group(1)
+        for h in range(2):
+            scale_rows(h)
+        value_turn(2, 2)
+        value_group(2)
+        for h in range(2):
+            quantize(table_q, half(h), flat(table_i[h][:]))
+        value_quantize(1)
+        value_quantize(0, "val_listed2")
+        value_quantize(2)
+        first = [products([0, 1], h, PACK + h) for h in range(2)]
+        third = [products([2], h, PACK + 2 + h) for h in range(2)]
+        res_lo = [tile([P, 2, H], F32, "res_lo%d" % h) for h in range(2)]
+        for h in range(2):
+            nc.vector.tensor_copy(res_lo[h][:], first[h][:])
+            nc.sync.dma_start(out_t[:, 0:2, half(h)], res_lo[h][:])
+        value_turn(3, PACK)
+        res_hi = [tile([P, 2, H], F32, "res_hi0", "val_win3"), tile([P, 2, H], F32, "res_hi1", "val_listed3")]
+        nc.scalar.copy(res_hi[0][:, 0:1, :], third[0][:])
+        value_group(3)
         value_quantize(3)
-        third = [products([2], h) for h in range(2)]
-        place(res_i[1], 0, res_lo[1][:])
-        nc.vector.tensor_copy(res_hi[0][:, 0:1, :], third[0][:])
         nc.scalar.copy(res_hi[1][:, 0:1, :], third[1][:])
         for h in range(2):
-            last = products([3], h)
+            place(res_i[h], 0, res_lo[h][:])
+        for h in range(2):
+            last = products([3], h, h)
             nc.scalar.copy(res_hi[h][:, 1:2, :], last[:])
             nc.sync.dma_start(out_t[:, 2:4, half(h)], res_hi[h][:])
             place(res_i[h], 1, res_hi[h][:])

from contextlib import ExitStack

import concourse.mybir as mybir
from concourse.masks import make_identity

D, T, I, J, U, Z, E = 512, 2048, 512, 512, 1024, 1024, 512
FLOPS = 2 * D * I * J * 2 + 2 * I * E * J

F32 = mybir.dt.float32
BF16 = mybir.dt.bfloat16
I32 = mybir.dt.int32
U32 = mybir.dt.uint32
U16 = mybir.dt.uint16
U8 = mybir.dt.uint8
FP8X4 = mybir.dt.float8_e4m3fn_x4
FP4X4 = mybir.dt.float4_e2m1fn_x4
COPY = mybir.ActivationFunctionType.Copy
MAX = mybir.AluOpType.max
MULT = mybir.AluOpType.mult

P = 128
PACK = 4
H = J // 2
LINE = 4


def tile_attend_tab_larger_exchange_pl_kernel(
    tc, keys_words, keys_scales, notes, users2, rowf, vals, offs, offs2, offs3, out_0, out_1, out_2
):
    nc = tc.nc
    with ExitStack() as ctx:
        lists = ctx.enter_context(tc.tile_pool(name="lists", bufs=1))
        sb = ctx.enter_context(tc.tile_pool(name="sb", bufs=1))
        ps = ctx.enter_context(tc.psum_pool(name="ps", bufs=1))

        def tile(shape, dtype, name, tag=None):
            return sb.tile(shape, dtype, name=name, tag=tag or name, align_bytes=64)

        def half(h):
            return slice(H * h, H * (h + 1))

        def half_list(h):
            return slice(H // 16 * h, H // 16 * (h + 1))

        tok_list = lists.tile([P, I // 16], U16, name="tok_list")
        note_list = lists.tile([P, J // 16], U16, name="note_list")
        user_list = lists.tile([P, J // 16], U16, name="user_list")

        key_words = tile([P, T], U16, "key_words")
        key_bytes = tile([P, T], U8, "key_bytes")
        note_win = [tile([P, U], F32, "note_win%d" % t) for t in range(PACK)]
        user_win = [tile([P, Z], F32, "user_win%d" % t) for t in range(PACK)]
        val_win = [tile([P, T], F32, "val_win%d" % t) for t in range(PACK)]
        factor = tile([P, PACK], F32, "factor")
        ident = tile([P, P], F32, "ident")

        make_identity(nc, ident[:])
        nc.sync.dma_start(factor[:], rowf.rearrange("(p r) o -> p (r o)", r=PACK))
        nc.sync.dma_start(tok_list[:], offs)
        for q in range(4):
            rows = keys_scales[0, 4 * q : 4 * q + 4, :].bitcast(I32)
            nc.sync.dma_start(key_bytes[32 * q : 32 * q + 32, :].bitcast(I32), rows.partition_broadcast(8))
        nc.sync.dma_start(key_words[:].bitcast(I32), keys_words[0].bitcast(I32))
        notes_t = notes.rearrange("(p t) u -> t p u", t=PACK)
        users_t = users2.rearrange("(p t) z -> t p z", t=PACK)
        vals_t = vals.rearrange("(m t) k -> t m k", t=PACK)
        nc.sync.dma_start(note_win[0][:], notes_t[0])
        nc.sync.dma_start(note_list[:], offs2)
        for t in range(1, PACK):
            nc.sync.dma_start(note_win[t][:], notes_t[t])
        nc.sync.dma_start(user_list[:], offs3)
        for t in range(PACK):
            nc.sync.dma_start(user_win[t][:], users_t[t])
        for t in range(PACK):
            nc.sync.dma_start(val_win[t][:], vals_t[t])

        factor_lines = tile([P, PACK, LINE], F32, "factor_lines")
        nc.scalar.copy(factor_lines[:], factor[:].unsqueeze(2).to_broadcast([P, PACK, LINE]))

        def bank(shape, b):
            return ps.tile(shape, F32, name="bank%d" % b, tag="bank%d" % b)

        def gather_vector(out, window, offsets):
            nc.vector.tensor_copy(out, window.indirect(offsets))

        def gather_scalar(out, window, offsets):
            nc.scalar.activation(out, window.indirect(offsets), COPY)

        def mx_tiles(name, width, tag=None):
            return tile([P, width], U32, name + "_codes", tag), tile([P, width], U8, name + "_scales")

        def quantize(operand, cols, grouped):
            codes, scales = operand
            nc.vector.quantize_mx(out=codes[:, cols].bitcast(FP8X4), scales=scales[:, cols], in_=grouped)

        def flat(grouped):
            return grouped.rearrange("p j t -> p (j t)")

        ks = tile([P, I], U8, "ks")
        gather_vector(ks[:].rearrange("p (r s) -> p s r", r=PACK), key_bytes[:], tok_list[:])
        kw_listed = tile([P, I], U16, "kw_listed")
        gather_vector(kw_listed[:], key_words[:], tok_list[:])
        kw = tile([P, I], U16, "kw")
        nc.vector.tensor_copy(
            kw[:].rearrange("p (r s) -> p r s", r=PACK), kw_listed[:].rearrange("p (s r) -> p r s", r=PACK)
        )

        def table(out, r, operand, cols):
            codes, scales = operand
            rows = slice(P * r, P * (r + 1))
            nc.tensor.matmul_mx(
                out,
                lhsT=kw[:, rows].bitcast(FP4X4),
                lhsT_scale=ks[:, rows],
                rhs=codes[:, cols].bitcast(FP8X4),
                rhs_scale=scales[:, cols],
                start=True,
                stop=True,
            )

        def place(grouped, pair, planes):
            nc.vector.tensor_copy(grouped[:, :, 2 * pair : 2 * pair + 2], planes.rearrange("p t j -> p j t"))

        note_g = tile([P, PACK, J], BF16, "note_g")
        note_i = tile([P, J, PACK], BF16, "note_i")
        note_q = mx_tiles("note", J)
        gather_scalar(note_g[:, 0, :], note_win[0][:], note_list[:])
        for t in range(1, PACK):
            gather_scalar(note_g[:, t, half(0)], note_win[t][:], note_list[:, half_list(0)])
            gather_vector(note_g[:, t, half(1)], note_win[t][:], note_list[:, half_list(1)])
        nc.vector.tensor_copy(
            note_i[:].rearrange("p (c i) t -> p c t i", i=LINE), note_g[:].rearrange("p t (c i) -> p c t i", i=LINE)
        )
        quantize(note_q, slice(0, J), flat(note_i[:]))

        user_lo = [tile([P, 2, H], BF16, "user_lo%d" % h) for h in range(2)]
        user_hi = [tile([P, 2, H], BF16, "user_hi%d" % h) for h in range(2)]
        user_i = [tile([P, H, PACK], BF16, "user_i%d" % h) for h in range(2)]
        user_q = mx_tiles("user", J)
        for h in range(2):
            gather_scalar(user_lo[h][:, 0, :], user_win[0][:], user_list[:, half_list(h)])
        gather_scalar(user_lo[0][:, 1, :], user_win[1][:], user_list[:, half_list(0)])
        gather_vector(user_lo[1][:, 1, :], user_win[1][:], user_list[:, half_list(1)])
        g1_banks = []
        for r in range(PACK):
            g1_banks.append(bank([P, J], r))
            table(g1_banks[r][:], r, note_q, slice(0, J))
        for h in range(2):
            gather_scalar(user_hi[h][:, 0, :], user_win[2][:], user_list[:, half_list(h)])
        for h in range(2):
            place(user_i[h], 0, user_lo[h][:])
        gather_scalar(user_hi[0][:, 1, :], user_win[3][:], user_list[:, half_list(0)])
        gather_vector(user_hi[1][:, 1, :], user_win[3][:], user_list[:, half_list(1)])
        g1 = tile([P, PACK, J], F32, "g1", "user_win3")
        for r in range(PACK):
            nc.scalar.copy(g1[:, r, :], g1_banks[r][:])
        for h in range(2):
            place(user_i[h], 1, user_hi[h][:])
        for h in range(2):
            quantize(user_q, half(h), flat(user_i[h][:]))

        turned = {}
        val_grouped = {}
        val_q = {}

        def value_turn(t, b):
            listed = tile([P, I], BF16, "val_listed%d" % t)
            gather_scalar(listed[:], val_win[t][:], tok_list[:])
            words = listed[:].bitcast(F32)
            turned[t] = bank([P, 2, P], b)
            for u in range(2):
                nc.tensor.transpose(turned[t][:, u, :], words[:, u : 2 * P : 2], ident[:])

        def value_group(t, tag=None):
            val_grouped[t] = tile([P, P * PACK], BF16, "val_grouped%d" % t, tag)
            nc.scalar.copy(
                val_grouped[t][:].bitcast(F32).rearrange("p (m u) -> p m u", u=2),
                turned[t][:].rearrange("p u m -> p m u"),
            )

        def value_quantize(t, tag=None):
            val_q[t] = mx_tiles("val%d" % t, P, tag)
            quantize(val_q[t], slice(0, P), val_grouped[t][:])

        larger = [tile([P, PACK, H], F32, "larger%d" % h) for h in range(2)]
        table_i = [tile([P, H, PACK], BF16, "table_i%d" % h) for h in range(2)]
        table_q = mx_tiles("table", J)

        g2_banks = {}
        for h in range(2):
            for pair in range(2):
                g2_banks[h, pair] = bank([P, 2, H], PACK + 2 * h + pair)
                for k in range(2):
                    table(g2_banks[h, pair][:, k, :], 2 * pair + k, user_q, half(h))

        def take_larger(h, pair):
            rows = slice(2 * pair, 2 * pair + 2)
            nc.vector.tensor_tensor(larger[h][:, rows, :], g2_banks[h, pair][:], g1[:, rows, half(h)], MAX)

        def scale_rows(h):
            nc.vector.tensor_tensor(
                table_i[h][:].rearrange("p (c i) r -> p c r i", i=LINE),
                larger[h][:].rearrange("p r (c i) -> p c r i", i=LINE),
                factor_lines[:].unsqueeze(1).to_broadcast([P, H // LINE, PACK, LINE]),
                MULT,
            )

        def products(planes, h, b):
            acc = bank([P, len(planes), H], b)
            for k, t in enumerate(planes):
                nc.tensor.matmul_mx(
                    acc[:, k, :],
                    lhsT=val_q[t][0][:].bitcast(FP8X4),
                    lhsT_scale=val_q[t][1][:],
                    rhs=table_q[0][:, half(h)].bitcast(FP8X4),
                    rhs_scale=table_q[1][:, half(h)],
                    start=True,
                    stop=True,
                )
            return acc

        res_i = [tile([P, H, PACK], BF16, "res_i%d" % h) for h in range(2)]
        res_q = mx_tiles("res", J)
        out_t = out_0.rearrange("(m t) j -> m t j", t=PACK)

        value_turn(0, 0)
        for h in range(2):
            for pair in range(2):
                take_larger(h, pair)
        value_turn(1, 1)
        value_group(0, "val_win1")
        value_group(1)
        for h in range(2):
            scale_rows(h)
        value_turn(2, 2)
        value_group(2)
        for h in range(2):
            quantize(table_q, half(h), flat(table_i[h][:]))
        value_quantize(1)
        value_quantize(0, "val_listed2")
        value_quantize(2)
        first = [products([0, 1], h, PACK + h) for h in range(2)]
        third = [products([2], h, PACK + 2 + h) for h in range(2)]
        res_lo = [tile([P, 2, H], F32, "res_lo%d" % h) for h in range(2)]
        for h in range(2):
            nc.vector.tensor_copy(res_lo[h][:], first[h][:])
            nc.sync.dma_start(out_t[:, 0:2, half(h)], res_lo[h][:])
        value_turn(3, PACK)
        res_hi = [tile([P, 2, H], F32, "res_hi0", "val_win3"), tile([P, 2, H], F32, "res_hi1", "val_listed3")]
        nc.scalar.copy(res_hi[0][:, 0:1, :], third[0][:])
        value_group(3)
        value_quantize(3)
        nc.scalar.copy(res_hi[1][:, 0:1, :], third[1][:])
        for h in range(2):
            place(res_i[h], 0, res_lo[h][:])
        for h in range(2):
            last = products([3], h, h)
            nc.scalar.copy(res_hi[h][:, 1:2, :], last[:])
            nc.sync.dma_start(out_t[:, 2:4, half(h)], res_hi[h][:])
            place(res_i[h], 1, res_hi[h][:])
        for h in range(2):
            quantize(res_q, half(h), flat(res_i[h][:]))
        nc.sync.dma_start(out_1[0].rearrange("p c r -> p (c r)").bitcast(I32), res_q[0][:].bitcast(I32))
        for r in range(4):
            queue = nc.sync if r % 2 == 0 else nc.scalar
            queue.dma_start(out_2[0, r:16:4, :].bitcast(I32), res_q[1][r:P:32, :].bitcast(I32))
